import numpy as np
import ml_dtypes


def mxq(x, axis, fmt="e4m3"):
    dtype, down = {"e4m3": (ml_dtypes.float8_e4m3fn, 7), "e5m2": (ml_dtypes.float8_e5m2, 14)}[fmt]
    v = np.moveaxis(np.asarray(x, np.float32).astype(ml_dtypes.bfloat16).astype(np.float64), axis, -1)
    blocks = v.reshape(v.shape[:-1] + (-1, 32))
    amax = np.abs(blocks).max(-1, keepdims=True)
    byte = np.maximum(np.where(amax > 0, np.frexp(amax)[1] - 1 + 127, 0) - down, 1)
    scale = np.exp2(byte - 127.0)
    codes = (blocks / scale).astype(np.float32).astype(dtype).astype(np.float64)
    return np.moveaxis((codes * scale).reshape(v.shape), -1, axis)


WIDE = False


def mx_kscale(k):
    if not WIDE:
        return np.ones(k)
    levels = np.array([10, -10, 5, -5, 0])
    if k % 512:
        return np.exp2(np.random.permutation(np.resize(levels, k // 32))).repeat(32)
    a = np.empty((k // 512, 16))
    for p in range(k // 512):
        a[p, :8] = np.random.permutation(np.resize(levels, 8))
        for g in range(8):
            far = levels[np.abs(levels - a[p, g]) >= 10]
            a[p, g + 8] = far[np.random.randint(len(far))]
    return np.exp2(a.ravel()).repeat(32)


def f64(x):
    return np.asarray(x).astype(np.float64)


def striped(idx):
    return np.tile(idx.reshape(-1, 16).T, (8, 1)).astype(np.uint16)


def unstriped(offs):
    return offs[:16].T.reshape(-1).astype(np.int64)


E2M1 = np.array([0.0, 0.5, 1.0, 1.5, 2.0, 3.0, 4.0, 6.0, -0.0, -0.5, -1.0, -1.5, -2.0, -3.0, -4.0, -6.0])


def pack_weight(w, fmt):
    k, n = w.shape
    w = f64(np.asarray(w, np.float32).astype(ml_dtypes.bfloat16)).reshape(k // 32, 32, n)
    amax = np.abs(w).max(1)
    if fmt == "e4m3":
        byte = np.frexp(amax)[1] - 1 + 127 - 7
    else:
        mant, ex = np.frexp(amax / 6.0)
        byte = np.where(mant > 0.5, ex, ex - 1) + 127
    byte = np.clip(np.where(amax > 0, byte, 1), 1, 254)
    scaled = (w * np.exp2(127.0 - byte)[:, None, :]).reshape(k, n).astype(np.float32)
    by_word = np.ascontiguousarray(scaled.reshape(k // 512, 128, 4, n).transpose(0, 1, 3, 2))
    if fmt == "e4m3":
        words = by_word.astype(ml_dtypes.float8_e4m3fn).view(np.uint8)
    else:
        c = by_word.astype(ml_dtypes.float4_e2m1fn).view(np.uint8) & 0xF
        words = (c[..., 0::2] | (c[..., 1::2] << 4)).reshape(k // 512, 128, 2 * n)
    return np.ascontiguousarray(words), np.ascontiguousarray(byte.astype(np.uint8).reshape(k // 512, 16, n))


def unpack_weight(words, scales, fmt):
    g, _, n = scales.shape
    words = np.ascontiguousarray(words).reshape(g, 128, n, -1)
    if fmt == "e4m3":
        vals = words.view(ml_dtypes.float8_e4m3fn).astype(np.float64)
    else:
        nib = np.empty((g, 128, n, 4), np.uint8)
        nib[..., 0::2] = words & 0xF
        nib[..., 1::2] = words >> 4
        vals = E2M1[nib]
    vals = vals * np.repeat(np.exp2(scales.astype(np.float64) - 127.0), 8, axis=1)[..., None]
    return vals.transpose(0, 1, 3, 2).reshape(g * 512, n)


def relu(v):
    return np.maximum(v, 0.0)


K, T, E, C, H, N = 512, 512, 12, 128, 512, 128
TOP = 3


def by_expert(wq, xq):
    return np.concatenate([wq[e].T @ xq[:, e * C:(e + 1) * C] for e in range(E)], axis=1)


def setup_inputs():
    n = np.random.standard_normal
    s = mx_kscale(K)[:, None]
    u = mx_kscale(H)
    deal = np.repeat(np.arange(E), C).reshape(TOP, T)[:, np.random.permutation(T)]
    deal = np.take_along_axis(deal, np.argsort(np.random.rand(TOP, T), axis=0), axis=0)
    for _ in range(8):
        s_, t_ = np.random.permutation(T).reshape(2, -1); r = np.random.randint(TOP, size=T // 2); x, y = deal[r, s_].copy(), deal[r, t_].copy()
        ok = ~((deal[:, s_] == y).any(0) | (deal[:, t_] == x).any(0)); deal[r[ok], s_[ok]] = y[ok]; deal[r[ok], t_[ok]] = x[ok]
    order = np.lexsort((np.random.rand(TOP * T), deal.reshape(-1)))
    slot_token = order % T; pos = np.empty(TOP * T, np.int64); pos[order] = np.arange(TOP * T); pos = pos.reshape(TOP, T)
    g = np.random.uniform(0.5, 1.5, (TOP, T)); g = g / g.sum(0)
    w1 = [pack_weight(m, "e2m1") for m in n((E, K, H)) / np.sqrt(K) / s[None]]
    w3 = [pack_weight(m, "e2m1") for m in n((E, K, H)) / np.sqrt(K) / s[None] * u[None, None, :]]
    w2 = [pack_weight(m, "e2m1") for m in n((E, H, N)) / np.sqrt(H) / u[None, :, None]]
    return {
        "xT": (n((K, T)) * s).astype(np.float32),
        "w1_words": np.stack([m[0] for m in w1]),
        "w1_scales": np.stack([m[1] for m in w1]),
        "w3_words": np.stack([m[0] for m in w3]),
        "w3_scales": np.stack([m[1] for m in w3]),
        "w2_words": np.stack([m[0] for m in w2]),
        "w2_scales": np.stack([m[1] for m in w2]),
        "gate": np.stack([np.tile(r, (N, 1)) for r in g]).astype(np.float32),
        "offs": striped(slot_token),
        "pos1": striped(pos[0]),
        "pos2": striped(pos[1]),
        "pos3": striped(pos[2]),
    }


def reference(xT, w1_words, w1_scales, w3_words, w3_scales, w2_words, w2_scales, gate, offs, pos1, pos2, pos3):
    idx = unstriped(offs)
    w1 = np.stack([unpack_weight(w1_words[e], w1_scales[e], "e2m1") for e in range(E)])
    w3 = np.stack([unpack_weight(w3_words[e], w3_scales[e], "e2m1") for e in range(E)])
    w2 = np.stack([unpack_weight(w2_words[e], w2_scales[e], "e2m1") for e in range(E)])
    xq = mxq(f64(xT)[:, idx], 0, "e4m3")
    h = relu(by_expert(w1, xq))
    h = h * by_expert(w3, xq)
    y = by_expert(w2, mxq(h, 0, "e4m3"))
    return sum(f64(gate[r]) * y[:, unstriped(p)] for r, p in enumerate((pos1, pos2, pos3)))

@@ -1,0 +1,218 @@
+from contextlib import ExitStack
+
+import concourse.mybir as mybir
+from concourse.masks import make_identity
+
+K, T, E, C, H, N = 512, 512, 12, 128, 512, 128
+TOP = 3
+P = 128
+S = E * C
+
+FLOPS = 2 * S * (2 * K * H + H * N)
+
+F32 = mybir.dt.float32
+BF16 = mybir.dt.bfloat16
+I32 = mybir.dt.int32
+U32 = mybir.dt.uint32
+U16 = mybir.dt.uint16
+U8 = mybir.dt.uint8
+FP8X4 = mybir.dt.float8_e4m3fn_x4
+FP4X4 = mybir.dt.float4_e2m1fn_x4
+MULT = mybir.AluOpType.mult
+ADD = mybir.AluOpType.add
+RELU = mybir.ActivationFunctionType.Relu
+
+GROUPS = [(0,), (1, 2), (3, 4), (5, 6), (7, 8), (9, 10), (11,)]
+X_CHUNKS = [(0, 256, 128), (256, 128, 64), (384, 128, 64)]
+PIECES = [(0, 1), (1, 3), (3, 6), (6, 9), (9, 12)]
+ON_GPSIMD = ()
+
+
+def tile_moe_tk_glu_relu_kernel(
+    tc, xT, w1_words, w1_scales, w3_words, w3_scales, w2_words, w2_scales, gate, offs, pos1, pos2, pos3, out
+):
+    nc = tc.nc
+    with ExitStack() as ctx:
+        held = ctx.enter_context(tc.tile_pool(name="held", bufs=1))
+        gathered = ctx.enter_context(tc.tile_pool(name="gathered", bufs=3))
+        work = ctx.enter_context(tc.tile_pool(name="work", bufs=4))
+        hidden = ctx.enter_context(tc.tile_pool(name="hidden", bufs=2))
+        psum_a = ctx.enter_context(tc.psum_pool(name="psum_a", bufs=2))
+        psum_b = ctx.enter_context(tc.psum_pool(name="psum_b", bufs=3))
+        psum_t = ctx.enter_context(tc.psum_pool(name="psum_t", bufs=2))
+        psum_y = ctx.enter_context(tc.psum_pool(name="psum_y", bufs=1))
+
+        offs_sb = held.tile([P, S // 16], U16, name="offs_sb")
+        nc.sync.dma_start(offs_sb[:], offs)
+
+        x_rows = xT.rearrange("(p j) t -> p j t", j=4)
+        x_f32 = []
+        for i, (t0, n, nv) in enumerate(X_CHUNKS):
+            xf = held.tile([P, 4, n], F32, name=f"x_f32_{i}")
+            nc.sync.dma_start(xf[:], x_rows[:, :, t0 : t0 + n])
+            x_f32.append(xf)
+
+        s1 = held.tile([P, E, H], U8, name="s1", align_bytes=64)
+        s3 = held.tile([P, E, H], U8, name="s3", align_bytes=64)
+        s2 = held.tile([P, E, N], U8, name="s2", align_bytes=64)
+        nc.vector.memset(s1[:, 0:3, :].rearrange("p e i -> p (e i)").bitcast(I32), 0)
+        nc.vector.memset(s3[:, 0:3, :].rearrange("p e i -> p (e i)").bitcast(I32), 0)
+        nc.vector.memset(s2[:].rearrange("p e i -> p (e i)").bitcast(I32), 0)
+        nc.vector.memset(s1[:, 3:E, :].rearrange("p e i -> p (e i)").bitcast(I32), 0)
+        nc.vector.memset(s3[:, 3:E, :].rearrange("p e i -> p (e i)").bitcast(I32), 0)
+
+        x_scales = held.tile([P, T], U8, name="x_scales", align_bytes=64)
+        nc.gpsimd.memset(x_scales[:], 0)
+
+        def load_scales(queue, plane, scales, e0, e1):
+            for q in range(4):
+                queue.dma_start(
+                    plane[32 * q : 32 * q + 4, e0:e1, :].bitcast(I32),
+                    scales[e0:e1, 0, 4 * q : 4 * q + 4, :].rearrange("e q i -> q e i").bitcast(I32),
+                )
+
+        w1_sb, w3_sb = {}, {}
+
+        def load_words(g):
+            e0, n = GROUPS[g][0], len(GROUPS[g])
+            for tag, words, held_words in (("w1", w1_words, w1_sb), ("w3", w3_words, w3_sb)):
+                w = held.tile([P, n, 2 * H], U8, name=f"{tag}_{g}", align_bytes=64)
+                nc.sync.dma_start(w[:].bitcast(I32), words[e0 : e0 + n, 0].rearrange("e p b -> p e b").bitcast(I32))
+                for k in range(n):
+                    held_words[e0 + k] = w[:, k, :]
+
+        load_words(0)
+        load_scales(nc.sync, s1, w1_scales, 0, 3)
+        load_scales(nc.gpsimd, s3, w3_scales, 0, 3)
+        load_words(1)
+        w2_sb = held.tile([P, E, 2 * N], U8, name="w2_sb", align_bytes=64)
+        load_scales(nc.sync, s2, w2_scales, 0, E)
+        nc.sync.dma_start(w2_sb[:].bitcast(I32), w2_words[:, 0].rearrange("e p b -> p e b").bitcast(I32))
+        load_scales(nc.sync, s1, w1_scales, 3, E)
+        load_scales(nc.sync, s3, w3_scales, 3, E)
+        for g in range(2, len(GROUPS)):
+            load_words(g)
+        pos_sb = []
+        for r, pos in enumerate((pos1, pos2, pos3)):
+            p_sb = held.tile([P, T // 16], U16, name=f"pos_sb_{r}")
+            nc.sync.dma_start(p_sb[:], pos)
+            pos_sb.append(p_sb)
+        gate_sb = held.tile([P, TOP, T], F32, name="gate_sb")
+        nc.sync.dma_start(gate_sb[:], gate.rearrange("r n t -> n r t"))
+
+        ident = held.tile([P, P], F32, name="ident")
+        make_identity(nc, ident[:])
+
+        x_words = held.tile([P, T], U32, name="x_words", align_bytes=64)
+        for i, (t0, n, nv) in enumerate(X_CHUNKS):
+            xf = x_f32[i]
+            xv = held.tile([P, nv, 4], BF16, name=f"xv_{i}", align_bytes=64)
+            xs = held.tile([P, n - nv, 4], BF16, name=f"xs_{i}", align_bytes=64)
+            nc.vector.tensor_copy(xv[:], xf[:, :, 0:nv].rearrange("p j t -> p t j"))
+            nc.scalar.copy(xs[:], xf[:, :, nv:n].rearrange("p j t -> p t j"))
+            for xb, a, b in ((xv, t0, t0 + nv), (xs, t0 + nv, t0 + n)):
+                nc.vector.quantize_mx(
+                    out=x_words[:, a:b].bitcast(FP8X4),
+                    scales=x_scales[:, a:b],
+                    in_=xb[:].rearrange("p t j -> p (t j)"),
+                )
+
+        y_all = held.tile([P, S], F32, name="y_all")
+        slots = {}
+
+        def gather(e0, e1):
+            n = e1 - e0
+            cols = offs_sb[:, e0 * C // 16 : (e0 + n) * C // 16]
+            words = gathered.tile([P, n * C], U32, name="words", align_bytes=64)
+            scales = gathered.tile([P, n * C], U8, name="scales", align_bytes=64)
+            nc.vector.tensor_copy(words[:], x_words[:].indirect(cols))
+            nc.vector.tensor_copy(scales[:], x_scales[:].indirect(cols))
+            for k in range(n):
+                slots[e0 + k] = (words[:, k * C : (k + 1) * C], scales[:, k * C : (k + 1) * C])
+
+        def order(ap):
+            return ap.rearrange("c (p u e) -> c u p e", u=2, e=2)
+
+        h_sb = {}
+
+        def first_layer(g):
+            for e in GROUPS[g]:
+                words, scales = slots[e]
+                a = psum_a.tile([C, H], F32, name="a")
+                b = psum_b.tile([C, H], F32, name="b")
+                for acc, w, s in ((a, w1_sb, s1), (b, w3_sb, s3)):
+                    nc.tensor.matmul_mx(
+                        out=acc[:],
+                        lhsT=words.bitcast(FP8X4),
+                        lhsT_scale=scales,
+                        rhs=w[e].bitcast(FP4X4),
+                        rhs_scale=s[:, e, :],
+                        start=True,
+                        stop=True,
+                    )
+                ra = work.tile([C, 2, P, 2], F32, name="ra")
+                nc.scalar.activation(ra[:], order(a[:]), RELU)
+                h = work.tile([C, 2, P, 2], BF16, name="h")
+                if e in ON_GPSIMD:
+                    rb = work.tile([C, 2, P, 2], F32, name="rb")
+                    nc.scalar.copy(rb[:], order(b[:]))
+                    nc.gpsimd.tensor_tensor(h[:], ra[:], rb[:], MULT)
+                else:
+                    nc.vector.tensor_tensor(h[:], order(b[:]), ra[:], MULT)
+                h_sb[e] = h
+
+        def second_layer(g):
+            e0, n = GROUPS[g][0], len(GROUPS[g])
+            tr = psum_t.tile([P, n, 2, C], F32, name="tr")
+            for k, e in enumerate(GROUPS[g]):
+                pairs = h_sb[e][:].rearrange("c u p e -> c (u p e)").bitcast(F32)
+                for u in range(2):
+                    nc.tensor.transpose(tr[:, k, u, :], pairs[:, u * P : (u + 1) * P], ident[:])
+            hT = hidden.tile([P, n, C, 4], BF16, name="hT", align_bytes=64)
+            nc.scalar.copy(hT[:].bitcast(F32), tr[:].rearrange("p k u c -> p k c u"))
+            hw = hidden.tile([P, n * C], U32, name="hw", align_bytes=64)
+            hs = hidden.tile([P, n * C], U8, name="hs", align_bytes=64)
+            nc.vector.quantize_mx(out=hw[:].bitcast(FP8X4), scales=hs[:], in_=hT[:].rearrange("p k c j -> p (k c j)"))
+            y = psum_y.tile([N, n * C], F32, name="y")
+            for k, e in enumerate(GROUPS[g]):
+                mine = slice(k * C, (k + 1) * C)
+                nc.tensor.matmul_mx(
+                    out=y[:, mine],
+                    lhsT=w2_sb[:, e, :].bitcast(FP4X4),
+                    lhsT_scale=s2[:, e, :],
+                    rhs=hw[:, mine].bitcast(FP8X4),
+                    rhs_scale=hs[:, mine],
+                    start=True,
+                    stop=True,
+                )
+            nc.scalar.copy(y_all[:, e0 * C : (e0 + n) * C], y[:])
+
+        gather(*PIECES[0])
+        gather(*PIECES[1])
+        first_layer(0)
+        for g in range(1, len(GROUPS)):
+            if g == 1 or g == 2 or g == 4:
+                gather(*PIECES[{1: 2, 2: 3, 4: 4}[g]])
+            first_layer(g)
+            second_layer(g - 1)
+        second_layer(len(GROUPS) - 1)
+
+        parts = [held.tile([P, T], F32, name=f"part_{r}") for r in range(TOP)]
+
+        def fetch(r, t0, t1):
+            nc.vector.tensor_tensor(
+                parts[r][:, t0:t1], y_all[:].indirect(pos_sb[r][:, t0 // 16 : t1 // 16]), gate_sb[:, r, t0:t1], MULT
+            )
+
+        half = T // 2
+        both = held.tile([P, T], F32, name="both")
+        total = held.tile([P, T], F32, name="total")
+        fetch(0, 0, T)
+        fetch(1, 0, T)
+        fetch(2, 0, half)
+        nc.vector.tensor_tensor(both[:], parts[0][:], parts[1][:], ADD)
+        fetch(2, half, T)
+        for t0 in (0, half):
+            cols = slice(t0, t0 + half)
+            nc.vector.tensor_tensor(total[:, cols], both[:, cols], parts[2][:, cols], ADD)
+            nc.sync.dma_start(out[:, cols], total[:, cols])

@@ -23,9 +23,11 @@ ADD = mybir.AluOpType.add
 RELU = mybir.ActivationFunctionType.Relu
 
 GROUPS = [(0,), (1, 2), (3, 4), (5, 6), (7, 8), (9, 10), (11,)]
-X_CHUNKS = [(0, 256, 128), (256, 128, 64), (384, 128, 64)]
-PIECES = [(0, 1), (1, 3), (3, 6), (6, 9), (9, 12)]
-ON_GPSIMD = ()
+X_CHUNKS = [(0, 256, "SV"), (256, 128, "S"), (384, 128, "V")]
+PIECES = [(0, 1), (1, 3), (3, 5), (5, 7), (7, 9), (9, 11), (11, 12)]
+ON_GPSIMD = (3, 5, 7)
+CUT1 = 3
+Y_BANKS = GROUPS
 
 
 def tile_moe_tk_glu_relu_kernel(
@@ -42,27 +44,28 @@ def tile_moe_tk_glu_relu_kernel(
         psum_t = ctx.enter_context(tc.psum_pool(name="psum_t", bufs=2))
         psum_y = ctx.enter_context(tc.psum_pool(name="psum_y", bufs=1))
 
-        offs_sb = held.tile([P, S // 16], U16, name="offs_sb")
-        nc.sync.dma_start(offs_sb[:], offs)
-
         x_rows = xT.rearrange("(p j) t -> p j t", j=4)
         x_f32 = []
-        for i, (t0, n, nv) in enumerate(X_CHUNKS):
+        for i, (t0, n, engines) in enumerate(X_CHUNKS):
             xf = held.tile([P, 4, n], F32, name=f"x_f32_{i}")
             nc.sync.dma_start(xf[:], x_rows[:, :, t0 : t0 + n])
             x_f32.append(xf)
+        offs_sb = held.tile([P, S // 16], U16, name="offs_sb")
+        nc.sync.dma_start(offs_sb[:], offs)
 
         s1 = held.tile([P, E, H], U8, name="s1", align_bytes=64)
         s3 = held.tile([P, E, H], U8, name="s3", align_bytes=64)
         s2 = held.tile([P, E, N], U8, name="s2", align_bytes=64)
-        nc.vector.memset(s1[:, 0:3, :].rearrange("p e i -> p (e i)").bitcast(I32), 0)
-        nc.vector.memset(s3[:, 0:3, :].rearrange("p e i -> p (e i)").bitcast(I32), 0)
-        nc.vector.memset(s2[:].rearrange("p e i -> p (e i)").bitcast(I32), 0)
-        nc.vector.memset(s1[:, 3:E, :].rearrange("p e i -> p (e i)").bitcast(I32), 0)
-        nc.vector.memset(s3[:, 3:E, :].rearrange("p e i -> p (e i)").bitcast(I32), 0)
+        for plane, e0, e1 in (
+            (s1, 0, CUT1), (s3, 0, CUT1), (s2, 0, E), (s1, CUT1, E), (s3, CUT1, E)
+        ):
+            nc.vector.memset(plane[:, e0:e1, :].rearrange("p e i -> p (e i)").bitcast(I32), 0)
 
         x_scales = held.tile([P, T], U8, name="x_scales", align_bytes=64)
         nc.gpsimd.memset(x_scales[:], 0)
+
+        ident = held.tile([P, P], F32, name="ident")
+        make_identity(nc, ident[:])
 
         def load_scales(queue, plane, scales, e0, e1):
             for q in range(4):
@@ -82,15 +85,16 @@ def tile_moe_tk_glu_relu_kernel(
                     held_words[e0 + k] = w[:, k, :]
 
         load_words(0)
-        load_scales(nc.sync, s1, w1_scales, 0, 3)
-        load_scales(nc.gpsimd, s3, w3_scales, 0, 3)
+        load_scales(nc.sync, s1, w1_scales, 0, CUT1)
+        load_scales(nc.gpsimd, s3, w3_scales, 0, CUT1)
         load_words(1)
         w2_sb = held.tile([P, E, 2 * N], U8, name="w2_sb", align_bytes=64)
         load_scales(nc.sync, s2, w2_scales, 0, E)
         nc.sync.dma_start(w2_sb[:].bitcast(I32), w2_words[:, 0].rearrange("e p b -> p e b").bitcast(I32))
-        load_scales(nc.sync, s1, w1_scales, 3, E)
-        load_scales(nc.sync, s3, w3_scales, 3, E)
-        for g in range(2, len(GROUPS)):
+        load_scales(nc.sync, s1, w1_scales, CUT1, E)
+        load_scales(nc.sync, s3, w3_scales, CUT1, E)
+        load_words(2)
+        for g in range(3, len(GROUPS)):
             load_words(g)
         pos_sb = []
         for r, pos in enumerate((pos1, pos2, pos3)):
@@ -100,22 +104,24 @@ def tile_moe_tk_glu_relu_kernel(
         gate_sb = held.tile([P, TOP, T], F32, name="gate_sb")
         nc.sync.dma_start(gate_sb[:], gate.rearrange("r n t -> n r t"))
 
-        ident = held.tile([P, P], F32, name="ident")
-        make_identity(nc, ident[:])
-
         x_words = held.tile([P, T], U32, name="x_words", align_bytes=64)
-        for i, (t0, n, nv) in enumerate(X_CHUNKS):
-            xf = x_f32[i]
-            xv = held.tile([P, nv, 4], BF16, name=f"xv_{i}", align_bytes=64)
-            xs = held.tile([P, n - nv, 4], BF16, name=f"xs_{i}", align_bytes=64)
-            nc.vector.tensor_copy(xv[:], xf[:, :, 0:nv].rearrange("p j t -> p t j"))
-            nc.scalar.copy(xs[:], xf[:, :, nv:n].rearrange("p j t -> p t j"))
-            for xb, a, b in ((xv, t0, t0 + nv), (xs, t0 + nv, t0 + n)):
-                nc.vector.quantize_mx(
-                    out=x_words[:, a:b].bitcast(FP8X4),
-                    scales=x_scales[:, a:b],
-                    in_=xb[:].rearrange("p t j -> p (t j)"),
-                )
+        x_bf16 = [held.tile([P, 256, 4], BF16, name=f"x_bf16_{i}", align_bytes=64) for i in range(2)]
+        for (t0, n, engines), xf in zip(X_CHUNKS, x_f32):
+            for k, engine in enumerate(engines):
+                rows = xf[:, :, 128 * k : 128 * (k + 1)].rearrange("p j t -> p t j")
+                a = (t0 + 128 * k) % 256
+                xb = x_bf16[t0 // 256][:, a : a + 128, :]
+                if engine == "S":
+                    nc.scalar.copy(xb, rows)
+                else:
+                    nc.vector.tensor_copy(xb, rows)
+        for i in range(2):
+            a, b = 256 * i, 256 * (i + 1)
+            nc.vector.quantize_mx(
+                out=x_words[:, a:b].bitcast(FP8X4),
+                scales=x_scales[:, a:b],
+                in_=x_bf16[i][:].rearrange("p t j -> p (t j)"),
+            )
 
         y_all = held.tile([P, S], F32, name="y_all")
         slots = {}
@@ -133,7 +139,7 @@ def tile_moe_tk_glu_relu_kernel(
         def order(ap):
             return ap.rearrange("c (p u e) -> c u p e", u=2, e=2)
 
-        h_sb = {}
+        h_sb, y_banks = {}, {}
 
         def first_layer(g):
             for e in GROUPS[g]:
@@ -169,15 +175,20 @@ def tile_moe_tk_glu_relu_kernel(
                 for u in range(2):
                     nc.tensor.transpose(tr[:, k, u, :], pairs[:, u * P : (u + 1) * P], ident[:])
             hT = hidden.tile([P, n, C, 4], BF16, name="hT", align_bytes=64)
-            nc.scalar.copy(hT[:].bitcast(F32), tr[:].rearrange("p k u c -> p k c u"))
+            last = g == len(GROUPS) - 1
+            empty = nc.vector.tensor_copy if last else nc.scalar.copy
+            empty(hT[:].bitcast(F32), tr[:].rearrange("p k u c -> p k c u"))
             hw = hidden.tile([P, n * C], U32, name="hw", align_bytes=64)
             hs = hidden.tile([P, n * C], U8, name="hs", align_bytes=64)
             nc.vector.quantize_mx(out=hw[:].bitcast(FP8X4), scales=hs[:], in_=hT[:].rearrange("p k c j -> p (k c j)"))
-            y = psum_y.tile([N, n * C], F32, name="y")
             for k, e in enumerate(GROUPS[g]):
                 mine = slice(k * C, (k + 1) * C)
+                bank = [b for b in Y_BANKS if e in b][0]
+                if e == bank[0]:
+                    y_banks[bank] = psum_y.tile([N, len(bank) * C], F32, name="y")
+                y = y_banks[bank]
                 nc.tensor.matmul_mx(
-                    out=y[:, mine],
+                    out=y[:, (e - bank[0]) * C : (e - bank[0] + 1) * C],
                     lhsT=w2_sb[:, e, :].bitcast(FP4X4),
                     lhsT_scale=s2[:, e, :],
                     rhs=hw[:, mine].bitcast(FP8X4),
@@ -185,16 +196,16 @@ def tile_moe_tk_glu_relu_kernel(
                     start=True,
                     stop=True,
                 )
-            nc.scalar.copy(y_all[:, e0 * C : (e0 + n) * C], y[:])
+                if e == bank[-1]:
+                    empty(y_all[:, bank[0] * C : (e + 1) * C], y[:])
 
         gather(*PIECES[0])
-        gather(*PIECES[1])
-        first_layer(0)
-        for g in range(1, len(GROUPS)):
-            if g == 1 or g == 2 or g == 4:
-                gather(*PIECES[{1: 2, 2: 3, 4: 4}[g]])
+        for g in range(len(GROUPS)):
+            if g > 0:
+                second_layer(g - 1)
             first_layer(g)
-            second_layer(g - 1)
+            if g + 1 < len(PIECES):
+                gather(*PIECES[g + 1])
         second_layer(len(GROUPS) - 1)
 
         parts = [held.tile([P, T], F32, name=f"part_{r}") for r in range(TOP)]
@@ -204,7 +215,7 @@ def tile_moe_tk_glu_relu_kernel(
                 parts[r][:, t0:t1], y_all[:].indirect(pos_sb[r][:, t0 // 16 : t1 // 16]), gate_sb[:, r, t0:t1], MULT
             )
 
-        half = T // 2
+        half = 384
         both = held.tile([P, T], F32, name="both")
         total = held.tile([P, T], F32, name="total")
         fetch(0, 0, T)
@@ -212,7 +223,7 @@ def tile_moe_tk_glu_relu_kernel(
         fetch(2, 0, half)
         nc.vector.tensor_tensor(both[:], parts[0][:], parts[1][:], ADD)
         fetch(2, half, T)
-        for t0 in (0, half):
-            cols = slice(t0, t0 + half)
+        for t0, t1 in ((0, half), (half, T)):
+            cols = slice(t0, t1)
             nc.vector.tensor_tensor(total[:, cols], both[:, cols], parts[2][:, cols], ADD)
             nc.sync.dma_start(out[:, cols], total[:, cols])

@@ -24,9 +24,11 @@ RELU = mybir.ActivationFunctionType.Relu
 
 GROUPS = [(0,), (1, 2), (3, 4), (5, 6), (7, 8), (9, 10), (11,)]
 X_CHUNKS = [(0, 256, "SV"), (256, 128, "S"), (384, 128, "V")]
-PIECES = [(0, 1), (1, 3), (3, 5), (5, 7), (7, 9), (9, 11), (11, 12)]
-ON_GPSIMD = (3, 5, 7)
+PIECES = [(0, 1), (1, 3), (3, 6), (6, 9), (9, 12)]
+ON_GPSIMD = (0, 1)
 CUT1 = 3
+W_GROUPS = [(0, 3), (3, 7), (7, 12)]
+T_ON_VECTOR = (3, 5, 6)
 Y_BANKS = GROUPS
 
 
@@ -36,7 +38,7 @@ def tile_moe_tk_glu_relu_kernel(
     nc = tc.nc
     with ExitStack() as ctx:
         held = ctx.enter_context(tc.tile_pool(name="held", bufs=1))
-        gathered = ctx.enter_context(tc.tile_pool(name="gathered", bufs=3))
+        gathered = ctx.enter_context(tc.tile_pool(name="gathered", bufs=5))
         work = ctx.enter_context(tc.tile_pool(name="work", bufs=4))
         hidden = ctx.enter_context(tc.tile_pool(name="hidden", bufs=2))
         psum_a = ctx.enter_context(tc.psum_pool(name="psum_a", bufs=2))
@@ -56,9 +58,7 @@ def tile_moe_tk_glu_relu_kernel(
         s1 = held.tile([P, E, H], U8, name="s1", align_bytes=64)
         s3 = held.tile([P, E, H], U8, name="s3", align_bytes=64)
         s2 = held.tile([P, E, N], U8, name="s2", align_bytes=64)
-        for plane, e0, e1 in (
-            (s1, 0, CUT1), (s3, 0, CUT1), (s2, 0, E), (s1, CUT1, E), (s3, CUT1, E)
-        ):
+        for plane, e0, e1 in ((s1, 0, CUT1), (s3, 0, CUT1), (s2, 0, E), (s1, CUT1, E)):
             nc.vector.memset(plane[:, e0:e1, :].rearrange("p e i -> p (e i)").bitcast(I32), 0)
 
         x_scales = held.tile([P, T], U8, name="x_scales", align_bytes=64)
@@ -77,24 +77,23 @@ def tile_moe_tk_glu_relu_kernel(
         w1_sb, w3_sb = {}, {}
 
         def load_words(g):
-            e0, n = GROUPS[g][0], len(GROUPS[g])
+            e0, e1 = W_GROUPS[g]
             for tag, words, held_words in (("w1", w1_words, w1_sb), ("w3", w3_words, w3_sb)):
-                w = held.tile([P, n, 2 * H], U8, name=f"{tag}_{g}", align_bytes=64)
-                nc.sync.dma_start(w[:].bitcast(I32), words[e0 : e0 + n, 0].rearrange("e p b -> p e b").bitcast(I32))
-                for k in range(n):
-                    held_words[e0 + k] = w[:, k, :]
+                w = held.tile([P, e1 - e0, 2 * H], U8, name=f"{tag}_{g}", align_bytes=64)
+                nc.sync.dma_start(w[:].bitcast(I32), words[e0:e1, 0].rearrange("e p b -> p e b").bitcast(I32))
+                for e in range(e0, e1):
+                    held_words[e] = w[:, e - e0, :]
 
-        load_words(0)
+        nc.gpsimd.memset(s3[:, CUT1:E, :].rearrange("p e i -> p (e i)").bitcast(I32), 0)
+        load_scales(nc.gpsimd, s3, w3_scales, CUT1, E)
         load_scales(nc.sync, s1, w1_scales, 0, CUT1)
-        load_scales(nc.gpsimd, s3, w3_scales, 0, CUT1)
-        load_words(1)
+        load_scales(nc.sync, s3, w3_scales, 0, CUT1)
+        load_words(0)
         w2_sb = held.tile([P, E, 2 * N], U8, name="w2_sb", align_bytes=64)
         load_scales(nc.sync, s2, w2_scales, 0, E)
         nc.sync.dma_start(w2_sb[:].bitcast(I32), w2_words[:, 0].rearrange("e p b -> p e b").bitcast(I32))
         load_scales(nc.sync, s1, w1_scales, CUT1, E)
-        load_scales(nc.sync, s3, w3_scales, CUT1, E)
-        load_words(2)
-        for g in range(3, len(GROUPS)):
+        for g in range(1, len(W_GROUPS)):
             load_words(g)
         pos_sb = []
         for r, pos in enumerate((pos1, pos2, pos3)):
@@ -176,8 +175,8 @@ def tile_moe_tk_glu_relu_kernel(
                     nc.tensor.transpose(tr[:, k, u, :], pairs[:, u * P : (u + 1) * P], ident[:])
             hT = hidden.tile([P, n, C, 4], BF16, name="hT", align_bytes=64)
             last = g == len(GROUPS) - 1
-            empty = nc.vector.tensor_copy if last else nc.scalar.copy
-            empty(hT[:].bitcast(F32), tr[:].rearrange("p k u c -> p k c u"))
+            empty = nc.vector.tensor_copy if g >= 5 else nc.scalar.copy
+            (nc.vector.tensor_copy if g in T_ON_VECTOR else nc.scalar.copy)(hT[:].bitcast(F32), tr[:].rearrange("p k u c -> p k c u"))
             hw = hidden.tile([P, n * C], U32, name="hw", align_bytes=64)
             hs = hidden.tile([P, n * C], U8, name="hs", align_bytes=64)
             nc.vector.quantize_mx(out=hw[:].bitcast(FP8X4), scales=hs[:], in_=hT[:].rearrange("p k c j -> p (k c j)"))
@@ -199,13 +198,12 @@ def tile_moe_tk_glu_relu_kernel(
                 if e == bank[-1]:
                     empty(y_all[:, bank[0] * C : (e + 1) * C], y[:])
 
-        gather(*PIECES[0])
+        for piece in PIECES:
+            gather(*piece)
         for g in range(len(GROUPS)):
             if g > 0:
                 second_layer(g - 1)
             first_layer(g)
-            if g + 1 < len(PIECES):
-                gather(*PIECES[g + 1])
         second_layer(len(GROUPS) - 1)
 
         parts = [held.tile([P, T], F32, name=f"part_{r}") for r in range(TOP)]

@@ -5,8 +5,9 @@ from concourse.masks import make_identity
 
 K, T, E, C, H, N = 512, 512, 12, 128, 512, 128
 TOP = 3
-P = 128
 S = E * C
+P = 128
+PACK = 4
 
 FLOPS = 2 * S * (2 * K * H + H * N)
 
@@ -23,13 +24,11 @@ ADD = mybir.AluOpType.add
 RELU = mybir.ActivationFunctionType.Relu
 
 GROUPS = [(0,), (1, 2), (3, 4), (5, 6), (7, 8), (9, 10), (11,)]
-X_CHUNKS = [(0, 256, "SV"), (256, 128, "S"), (384, 128, "V")]
 PIECES = [(0, 1), (1, 3), (3, 6), (6, 9), (9, 12)]
-ON_GPSIMD = (0, 1)
-CUT1 = 3
-W_GROUPS = [(0, 3), (3, 7), (7, 12)]
-T_ON_VECTOR = (3, 5, 6)
-Y_BANKS = GROUPS
+EARLY = 3
+X_CHUNKS = [(0, 256, ("scalar", "vector")), (256, 128, ("scalar",)), (384, 128, ("vector",))]
+X_TILE = 256
+CUT = 384
 
 
 def tile_moe_tk_glu_relu_kernel(
@@ -38,190 +37,182 @@ def tile_moe_tk_glu_relu_kernel(
     nc = tc.nc
     with ExitStack() as ctx:
         held = ctx.enter_context(tc.tile_pool(name="held", bufs=1))
-        gathered = ctx.enter_context(tc.tile_pool(name="gathered", bufs=5))
-        work = ctx.enter_context(tc.tile_pool(name="work", bufs=4))
-        hidden = ctx.enter_context(tc.tile_pool(name="hidden", bufs=2))
-        psum_a = ctx.enter_context(tc.psum_pool(name="psum_a", bufs=2))
-        psum_b = ctx.enter_context(tc.psum_pool(name="psum_b", bufs=3))
-        psum_t = ctx.enter_context(tc.psum_pool(name="psum_t", bufs=2))
-        psum_y = ctx.enter_context(tc.psum_pool(name="psum_y", bufs=1))
-
-        x_rows = xT.rearrange("(p j) t -> p j t", j=4)
-        x_f32 = []
-        for i, (t0, n, engines) in enumerate(X_CHUNKS):
-            xf = held.tile([P, 4, n], F32, name=f"x_f32_{i}")
-            nc.sync.dma_start(xf[:], x_rows[:, :, t0 : t0 + n])
-            x_f32.append(xf)
-        offs_sb = held.tile([P, S // 16], U16, name="offs_sb")
-        nc.sync.dma_start(offs_sb[:], offs)
+        gathered = ctx.enter_context(tc.tile_pool(name="gathered", bufs=3))
+        products = ctx.enter_context(tc.tile_pool(name="products", bufs=6))
+        hidden = ctx.enter_context(tc.tile_pool(name="hidden", bufs=4))
+        psum = ctx.enter_context(tc.psum_pool(name="psum", bufs=2))
 
         s1 = held.tile([P, E, H], U8, name="s1", align_bytes=64)
         s3 = held.tile([P, E, H], U8, name="s3", align_bytes=64)
         s2 = held.tile([P, E, N], U8, name="s2", align_bytes=64)
-        for plane, e0, e1 in ((s1, 0, CUT1), (s3, 0, CUT1), (s2, 0, E), (s1, CUT1, E)):
-            nc.vector.memset(plane[:, e0:e1, :].rearrange("p e i -> p (e i)").bitcast(I32), 0)
-
+        x_words = held.tile([P, T], U32, name="x_words", align_bytes=64)
         x_scales = held.tile([P, T], U8, name="x_scales", align_bytes=64)
-        nc.gpsimd.memset(x_scales[:], 0)
-
         ident = held.tile([P, P], F32, name="ident")
+
+        def zero(engine, scales, e0, e1):
+            engine.memset(scales[:, e0:e1, :].rearrange("p e i -> p (e i)").bitcast(I32), 0)
+
+        zero(nc.vector, s1, 0, EARLY)
+        zero(nc.vector, s3, 0, EARLY)
+        zero(nc.vector, s2, 0, E)
+        nc.gpsimd.memset(x_scales[:], 0)
+        zero(nc.gpsimd, s1, EARLY, E)
+        zero(nc.gpsimd, s3, EARLY, E)
         make_identity(nc, ident[:])
 
-        def load_scales(queue, plane, scales, e0, e1):
+        x_rows = xT.rearrange("(p j) t -> p j t", j=PACK)
+        x_f32 = []
+        for i, (t0, n, engines) in enumerate(X_CHUNKS):
+            chunk = held.tile([P, PACK, n], F32, name=f"x_f32_{i}")
+            nc.sync.dma_start(chunk[:], x_rows[:, :, t0 : t0 + n])
+            x_f32.append(chunk)
+        offs_sb = held.tile([P, S // 16], U16, name="offs_sb")
+        nc.sync.dma_start(offs_sb[:], offs)
+
+        def load_scales(tile, scales, e0, e1):
             for q in range(4):
-                queue.dma_start(
-                    plane[32 * q : 32 * q + 4, e0:e1, :].bitcast(I32),
+                nc.sync.dma_start(
+                    tile[32 * q : 32 * q + 4, e0:e1, :].bitcast(I32),
                     scales[e0:e1, 0, 4 * q : 4 * q + 4, :].rearrange("e q i -> q e i").bitcast(I32),
                 )
 
         w1_sb, w3_sb = {}, {}
 
         def load_words(g):
-            e0, e1 = W_GROUPS[g]
-            for tag, words, held_words in (("w1", w1_words, w1_sb), ("w3", w3_words, w3_sb)):
-                w = held.tile([P, e1 - e0, 2 * H], U8, name=f"{tag}_{g}", align_bytes=64)
-                nc.sync.dma_start(w[:].bitcast(I32), words[e0:e1, 0].rearrange("e p b -> p e b").bitcast(I32))
-                for e in range(e0, e1):
-                    held_words[e] = w[:, e - e0, :]
+            for name, words, by_expert in ((f"w1_{g}", w1_words, w1_sb), (f"w3_{g}", w3_words, w3_sb)):
+                e0, n = GROUPS[g][0], len(GROUPS[g])
+                w = held.tile([P, n, 2 * H], U8, name=name, align_bytes=64)
+                nc.sync.dma_start(w[:].bitcast(I32), words[e0 : e0 + n, 0].rearrange("e p b -> p e b").bitcast(I32))
+                for k in range(n):
+                    by_expert[e0 + k] = w[:, k, :]
 
-        nc.gpsimd.memset(s3[:, CUT1:E, :].rearrange("p e i -> p (e i)").bitcast(I32), 0)
-        load_scales(nc.gpsimd, s3, w3_scales, CUT1, E)
-        load_scales(nc.sync, s1, w1_scales, 0, CUT1)
-        load_scales(nc.sync, s3, w3_scales, 0, CUT1)
         load_words(0)
+        load_scales(s1, w1_scales, 0, EARLY)
+        load_scales(s3, w3_scales, 0, EARLY)
+        load_words(1)
+        load_scales(s2, w2_scales, 0, E)
         w2_sb = held.tile([P, E, 2 * N], U8, name="w2_sb", align_bytes=64)
-        load_scales(nc.sync, s2, w2_scales, 0, E)
         nc.sync.dma_start(w2_sb[:].bitcast(I32), w2_words[:, 0].rearrange("e p b -> p e b").bitcast(I32))
-        load_scales(nc.sync, s1, w1_scales, CUT1, E)
-        for g in range(1, len(W_GROUPS)):
+        load_scales(s1, w1_scales, EARLY, E)
+        load_scales(s3, w3_scales, EARLY, E)
+        for g in range(2, len(GROUPS)):
             load_words(g)
         pos_sb = []
         for r, pos in enumerate((pos1, pos2, pos3)):
-            p_sb = held.tile([P, T // 16], U16, name=f"pos_sb_{r}")
-            nc.sync.dma_start(p_sb[:], pos)
-            pos_sb.append(p_sb)
+            places = held.tile([P, T // 16], U16, name=f"pos_sb_{r}")
+            nc.sync.dma_start(places[:], pos)
+            pos_sb.append(places)
         gate_sb = held.tile([P, TOP, T], F32, name="gate_sb")
         nc.sync.dma_start(gate_sb[:], gate.rearrange("r n t -> n r t"))
 
-        x_words = held.tile([P, T], U32, name="x_words", align_bytes=64)
-        x_bf16 = [held.tile([P, 256, 4], BF16, name=f"x_bf16_{i}", align_bytes=64) for i in range(2)]
-        for (t0, n, engines), xf in zip(X_CHUNKS, x_f32):
+        x_bf16 = [held.tile([P, X_TILE, PACK], BF16, name=f"x_bf16_{i}", align_bytes=64) for i in range(T // X_TILE)]
+        for (t0, n, engines), chunk in zip(X_CHUNKS, x_f32):
             for k, engine in enumerate(engines):
-                rows = xf[:, :, 128 * k : 128 * (k + 1)].rearrange("p j t -> p t j")
-                a = (t0 + 128 * k) % 256
-                xb = x_bf16[t0 // 256][:, a : a + 128, :]
-                if engine == "S":
-                    nc.scalar.copy(xb, rows)
+                rounded = x_bf16[t0 // X_TILE][:, t0 % X_TILE + 128 * k : t0 % X_TILE + 128 * (k + 1), :]
+                rows = chunk[:, :, 128 * k : 128 * (k + 1)].rearrange("p j t -> p t j")
+                if engine == "scalar":
+                    nc.scalar.copy(rounded, rows)
                 else:
-                    nc.vector.tensor_copy(xb, rows)
-        for i in range(2):
-            a, b = 256 * i, 256 * (i + 1)
+                    nc.vector.tensor_copy(rounded, rows)
+        for i, rounded in enumerate(x_bf16):
+            cols = slice(X_TILE * i, X_TILE * (i + 1))
             nc.vector.quantize_mx(
-                out=x_words[:, a:b].bitcast(FP8X4),
-                scales=x_scales[:, a:b],
-                in_=x_bf16[i][:].rearrange("p t j -> p (t j)"),
+                out=x_words[:, cols].bitcast(FP8X4),
+                scales=x_scales[:, cols],
+                in_=rounded[:].rearrange("p t j -> p (t j)"),
             )
 
-        y_all = held.tile([P, S], F32, name="y_all")
-        slots = {}
+        codes_of, scales_of = {}, {}
 
         def gather(e0, e1):
             n = e1 - e0
-            cols = offs_sb[:, e0 * C // 16 : (e0 + n) * C // 16]
-            words = gathered.tile([P, n * C], U32, name="words", align_bytes=64)
+            listed = offs_sb[:, e0 * C // 16 : e1 * C // 16]
+            codes = gathered.tile([P, n * C], U32, name="codes", align_bytes=64)
             scales = gathered.tile([P, n * C], U8, name="scales", align_bytes=64)
-            nc.vector.tensor_copy(words[:], x_words[:].indirect(cols))
-            nc.vector.tensor_copy(scales[:], x_scales[:].indirect(cols))
+            nc.vector.tensor_copy(codes[:], x_words[:].indirect(listed))
+            nc.vector.tensor_copy(scales[:], x_scales[:].indirect(listed))
             for k in range(n):
-                slots[e0 + k] = (words[:, k * C : (k + 1) * C], scales[:, k * C : (k + 1) * C])
+                codes_of[e0 + k] = codes[:, k * C : (k + 1) * C]
+                scales_of[e0 + k] = scales[:, k * C : (k + 1) * C]
 
-        def order(ap):
-            return ap.rearrange("c (p u e) -> c u p e", u=2, e=2)
+        def by_pairs(acc):
+            return acc.rearrange("c (p u v) -> c u p v", u=2, v=2)
 
-        h_sb, y_banks = {}, {}
+        h_of = {}
 
         def first_layer(g):
             for e in GROUPS[g]:
-                words, scales = slots[e]
-                a = psum_a.tile([C, H], F32, name="a")
-                b = psum_b.tile([C, H], F32, name="b")
+                a = psum.tile([C, H], F32, name="a")
+                b = psum.tile([C, H], F32, name="b")
                 for acc, w, s in ((a, w1_sb, s1), (b, w3_sb, s3)):
                     nc.tensor.matmul_mx(
                         out=acc[:],
-                        lhsT=words.bitcast(FP8X4),
-                        lhsT_scale=scales,
+                        lhsT=codes_of[e].bitcast(FP8X4),
+                        lhsT_scale=scales_of[e],
                         rhs=w[e].bitcast(FP4X4),
                         rhs_scale=s[:, e, :],
                         start=True,
                         stop=True,
                     )
-                ra = work.tile([C, 2, P, 2], F32, name="ra")
-                nc.scalar.activation(ra[:], order(a[:]), RELU)
-                h = work.tile([C, 2, P, 2], BF16, name="h")
-                if e in ON_GPSIMD:
-                    rb = work.tile([C, 2, P, 2], F32, name="rb")
-                    nc.scalar.copy(rb[:], order(b[:]))
-                    nc.gpsimd.tensor_tensor(h[:], ra[:], rb[:], MULT)
-                else:
-                    nc.vector.tensor_tensor(h[:], order(b[:]), ra[:], MULT)
-                h_sb[e] = h
+                relu_a = products.tile([C, 2, P, 2], F32, name="relu_a")
+                nc.scalar.activation(relu_a[:], by_pairs(a[:]), RELU)
+                h = products.tile([C, 2, P, 2], BF16, name="h")
+                nc.vector.tensor_tensor(h[:], by_pairs(b[:]), relu_a[:], MULT)
+                h_of[e] = h
+
+        y_all = held.tile([N, S], F32, name="y_all")
 
         def second_layer(g):
             e0, n = GROUPS[g][0], len(GROUPS[g])
-            tr = psum_t.tile([P, n, 2, C], F32, name="tr")
+            empty = nc.vector.tensor_copy if g == len(GROUPS) - 1 else nc.scalar.copy
+
+            turned = psum.tile([P, n, 2, C], F32, name="turned")
             for k, e in enumerate(GROUPS[g]):
-                pairs = h_sb[e][:].rearrange("c u p e -> c (u p e)").bitcast(F32)
+                words = h_of[e][:].rearrange("c u p v -> c (u p v)").bitcast(F32)
                 for u in range(2):
-                    nc.tensor.transpose(tr[:, k, u, :], pairs[:, u * P : (u + 1) * P], ident[:])
-            hT = hidden.tile([P, n, C, 4], BF16, name="hT", align_bytes=64)
-            last = g == len(GROUPS) - 1
-            empty = nc.vector.tensor_copy if g >= 5 else nc.scalar.copy
-            (nc.vector.tensor_copy if g in T_ON_VECTOR else nc.scalar.copy)(hT[:].bitcast(F32), tr[:].rearrange("p k u c -> p k c u"))
-            hw = hidden.tile([P, n * C], U32, name="hw", align_bytes=64)
-            hs = hidden.tile([P, n * C], U8, name="hs", align_bytes=64)
-            nc.vector.quantize_mx(out=hw[:].bitcast(FP8X4), scales=hs[:], in_=hT[:].rearrange("p k c j -> p (k c j)"))
+                    nc.tensor.transpose(turned[:, k, u, :], words[:, u * P : (u + 1) * P], ident[:])
+            h_rows = hidden.tile([P, n, C, PACK], BF16, name="h_rows", align_bytes=64)
+            empty(h_rows[:].bitcast(F32), turned[:].rearrange("p k u c -> p k c u"))
+
+            h_codes = hidden.tile([P, n * C], U32, name="h_codes", align_bytes=64)
+            h_scales = hidden.tile([P, n * C], U8, name="h_scales", align_bytes=64)
+            nc.vector.quantize_mx(
+                out=h_codes[:].bitcast(FP8X4),
+                scales=h_scales[:],
+                in_=h_rows[:].rearrange("p k c j -> p (k c j)"),
+            )
+            y = psum.tile([N, n * C], F32, name="y")
             for k, e in enumerate(GROUPS[g]):
                 mine = slice(k * C, (k + 1) * C)
-                bank = [b for b in Y_BANKS if e in b][0]
-                if e == bank[0]:
-                    y_banks[bank] = psum_y.tile([N, len(bank) * C], F32, name="y")
-                y = y_banks[bank]
                 nc.tensor.matmul_mx(
-                    out=y[:, (e - bank[0]) * C : (e - bank[0] + 1) * C],
+                    out=y[:, mine],
                     lhsT=w2_sb[:, e, :].bitcast(FP4X4),
                     lhsT_scale=s2[:, e, :],
-                    rhs=hw[:, mine].bitcast(FP8X4),
-                    rhs_scale=hs[:, mine],
+                    rhs=h_codes[:, mine].bitcast(FP8X4),
+                    rhs_scale=h_scales[:, mine],
                     start=True,
                     stop=True,
                 )
-                if e == bank[-1]:
-                    empty(y_all[:, bank[0] * C : (e + 1) * C], y[:])
+            empty(y_all[:, e0 * C : (e0 + n) * C], y[:])
 
-        for piece in PIECES:
-            gather(*piece)
+        fetched = 0
         for g in range(len(GROUPS)):
+            ahead = GROUPS[min(g + 1, len(GROUPS) - 1)][-1]
+            for e0, e1 in PIECES:
+                if fetched == e0 and e0 <= ahead:
+                    gather(e0, e1)
+                    fetched = e1
+            first_layer(g)
             if g > 0:
                 second_layer(g - 1)
-            first_layer(g)
         second_layer(len(GROUPS) - 1)
 
-        parts = [held.tile([P, T], F32, name=f"part_{r}") for r in range(TOP)]
-
-        def fetch(r, t0, t1):
-            nc.vector.tensor_tensor(
-                parts[r][:, t0:t1], y_all[:].indirect(pos_sb[r][:, t0 // 16 : t1 // 16]), gate_sb[:, r, t0:t1], MULT
-            )
-
-        half = 384
-        both = held.tile([P, T], F32, name="both")
-        total = held.tile([P, T], F32, name="total")
-        fetch(0, 0, T)
-        fetch(1, 0, T)
-        fetch(2, 0, half)
-        nc.vector.tensor_tensor(both[:], parts[0][:], parts[1][:], ADD)
-        fetch(2, half, T)
-        for t0, t1 in ((0, half), (half, T)):
-            cols = slice(t0, t1)
-            nc.vector.tensor_tensor(total[:, cols], both[:, cols], parts[2][:, cols], ADD)
-            nc.sync.dma_start(out[:, cols], total[:, cols])
+        parts = [held.tile([N, T], F32, name=f"part_{r}") for r in range(TOP)]
+        for r in range(TOP):
+            nc.vector.tensor_tensor(parts[r][:], y_all[:].indirect(pos_sb[r][:]), gate_sb[:, r, :], MULT)
+        two = held.tile([N, T], F32, name="two")
+        total = held.tile([N, T], F32, name="total")
+        nc.vector.tensor_tensor(two[:], parts[0][:], parts[1][:], ADD)
+        for t0, t1 in ((0, CUT), (CUT, T)):
+            nc.vector.tensor_tensor(total[:, t0:t1], two[:, t0:t1], parts[2][:, t0:t1], ADD)
+            nc.sync.dma_start(out[:, t0:t1], total[:, t0:t1])

from contextlib import ExitStack

import concourse.mybir as mybir
from concourse.masks import make_identity

K, T, E, C, H, N = 512, 512, 12, 128, 512, 128
TOP = 3
S = E * C
P = 128
PACK = 4

FLOPS = 2 * S * (2 * K * H + H * N)

F32 = mybir.dt.float32
BF16 = mybir.dt.bfloat16
I32 = mybir.dt.int32
U32 = mybir.dt.uint32
U16 = mybir.dt.uint16
U8 = mybir.dt.uint8
FP8X4 = mybir.dt.float8_e4m3fn_x4
FP4X4 = mybir.dt.float4_e2m1fn_x4
MULT = mybir.AluOpType.mult
ADD = mybir.AluOpType.add
RELU = mybir.ActivationFunctionType.Relu

GROUPS = [(0,), (1, 2), (3, 4), (5, 6), (7, 8), (9, 10), (11,)]
PIECES = [(0, 1), (1, 3), (3, 6), (6, 9), (9, 12)]
EARLY = 3
X_CHUNKS = [(0, 256, ("scalar", "vector")), (256, 128, ("scalar",)), (384, 128, ("vector",))]
X_TILE = 256
CUT = 384


def tile_moe_tk_glu_relu_kernel(
    tc, xT, w1_words, w1_scales, w3_words, w3_scales, w2_words, w2_scales, gate, offs, pos1, pos2, pos3, out
):
    nc = tc.nc
    with ExitStack() as ctx:
        held = ctx.enter_context(tc.tile_pool(name="held", bufs=1))
        gathered = ctx.enter_context(tc.tile_pool(name="gathered", bufs=3))
        products = ctx.enter_context(tc.tile_pool(name="products", bufs=6))
        hidden = ctx.enter_context(tc.tile_pool(name="hidden", bufs=4))
        psum = ctx.enter_context(tc.psum_pool(name="psum", bufs=2))

        s1 = held.tile([P, E, H], U8, name="s1", align_bytes=64)
        s3 = held.tile([P, E, H], U8, name="s3", align_bytes=64)
        s2 = held.tile([P, E, N], U8, name="s2", align_bytes=64)
        x_words = held.tile([P, T], U32, name="x_words", align_bytes=64)
        x_scales = held.tile([P, T], U8, name="x_scales", align_bytes=64)
        ident = held.tile([P, P], F32, name="ident")

        def zero(engine, scales, e0, e1):
            engine.memset(scales[:, e0:e1, :].rearrange("p e i -> p (e i)").bitcast(I32), 0)

        zero(nc.vector, s1, 0, EARLY)
        zero(nc.vector, s3, 0, EARLY)
        zero(nc.vector, s2, 0, E)
        nc.gpsimd.memset(x_scales[:], 0)
        zero(nc.gpsimd, s1, EARLY, E)
        zero(nc.gpsimd, s3, EARLY, E)
        make_identity(nc, ident[:])

        x_rows = xT.rearrange("(p j) t -> p j t", j=PACK)
        x_f32 = []
        for i, (t0, n, engines) in enumerate(X_CHUNKS):
            chunk = held.tile([P, PACK, n], F32, name=f"x_f32_{i}")
            nc.sync.dma_start(chunk[:], x_rows[:, :, t0 : t0 + n])
            x_f32.append(chunk)
        offs_sb = held.tile([P, S // 16], U16, name="offs_sb")
        nc.sync.dma_start(offs_sb[:], offs)

        def load_scales(tile, scales, e0, e1):
            for q in range(4):
                nc.sync.dma_start(
                    tile[32 * q : 32 * q + 4, e0:e1, :].bitcast(I32),
                    scales[e0:e1, 0, 4 * q : 4 * q + 4, :].rearrange("e q i -> q e i").bitcast(I32),
                )

        w1_sb, w3_sb = {}, {}

        def load_words(g):
            for name, words, by_expert in ((f"w1_{g}", w1_words, w1_sb), (f"w3_{g}", w3_words, w3_sb)):
                e0, n = GROUPS[g][0], len(GROUPS[g])
                w = held.tile([P, n, 2 * H], U8, name=name, align_bytes=64)
                nc.sync.dma_start(w[:].bitcast(I32), words[e0 : e0 + n, 0].rearrange("e p b -> p e b").bitcast(I32))
                for k in range(n):
                    by_expert[e0 + k] = w[:, k, :]

        load_words(0)
        load_scales(s1, w1_scales, 0, EARLY)
        load_scales(s3, w3_scales, 0, EARLY)
        load_words(1)
        load_scales(s2, w2_scales, 0, E)
        w2_sb = held.tile([P, E, 2 * N], U8, name="w2_sb", align_bytes=64)
        nc.sync.dma_start(w2_sb[:].bitcast(I32), w2_words[:, 0].rearrange("e p b -> p e b").bitcast(I32))
        load_scales(s1, w1_scales, EARLY, E)
        load_scales(s3, w3_scales, EARLY, E)
        for g in range(2, len(GROUPS)):
            load_words(g)
        pos_sb = []
        for r, pos in enumerate((pos1, pos2, pos3)):
            places = held.tile([P, T // 16], U16, name=f"pos_sb_{r}")
            nc.sync.dma_start(places[:], pos)
            pos_sb.append(places)
        gate_sb = held.tile([P, TOP, T], F32, name="gate_sb")
        nc.sync.dma_start(gate_sb[:], gate.rearrange("r n t -> n r t"))

        x_bf16 = [held.tile([P, X_TILE, PACK], BF16, name=f"x_bf16_{i}", align_bytes=64) for i in range(T // X_TILE)]
        for (t0, n, engines), chunk in zip(X_CHUNKS, x_f32):
            for k, engine in enumerate(engines):
                rounded = x_bf16[t0 // X_TILE][:, t0 % X_TILE + 128 * k : t0 % X_TILE + 128 * (k + 1), :]
                rows = chunk[:, :, 128 * k : 128 * (k + 1)].rearrange("p j t -> p t j")
                if engine == "scalar":
                    nc.scalar.copy(rounded, rows)
                else:
                    nc.vector.tensor_copy(rounded, rows)
        for i, rounded in enumerate(x_bf16):
            cols = slice(X_TILE * i, X_TILE * (i + 1))
            nc.vector.quantize_mx(
                out=x_words[:, cols].bitcast(FP8X4),
                scales=x_scales[:, cols],
                in_=rounded[:].rearrange("p t j -> p (t j)"),
            )

        codes_of, scales_of = {}, {}

        def gather(e0, e1):
            n = e1 - e0
            listed = offs_sb[:, e0 * C // 16 : e1 * C // 16]
            codes = gathered.tile([P, n * C], U32, name="codes", align_bytes=64)
            scales = gathered.tile([P, n * C], U8, name="scales", align_bytes=64)
            nc.vector.tensor_copy(codes[:], x_words[:].indirect(listed))
            nc.vector.tensor_copy(scales[:], x_scales[:].indirect(listed))
            for k in range(n):
                codes_of[e0 + k] = codes[:, k * C : (k + 1) * C]
                scales_of[e0 + k] = scales[:, k * C : (k + 1) * C]

        def by_pairs(acc):
            return acc.rearrange("c (p u v) -> c u p v", u=2, v=2)

        h_of = {}

        def first_layer(g):
            for e in GROUPS[g]:
                a = psum.tile([C, H], F32, name="a")
                b = psum.tile([C, H], F32, name="b")
                for acc, w, s in ((a, w1_sb, s1), (b, w3_sb, s3)):
                    nc.tensor.matmul_mx(
                        out=acc[:],
                        lhsT=codes_of[e].bitcast(FP8X4),
                        lhsT_scale=scales_of[e],
                        rhs=w[e].bitcast(FP4X4),
                        rhs_scale=s[:, e, :],
                        start=True,
                        stop=True,
                    )
                relu_a = products.tile([C, 2, P, 2], F32, name="relu_a")
                nc.scalar.activation(relu_a[:], by_pairs(a[:]), RELU)
                h = products.tile([C, 2, P, 2], BF16, name="h")
                nc.vector.tensor_tensor(h[:], by_pairs(b[:]), relu_a[:], MULT)
                h_of[e] = h

        y_all = held.tile([N, S], F32, name="y_all")

        def second_layer(g):
            e0, n = GROUPS[g][0], len(GROUPS[g])
            empty = nc.vector.tensor_copy if g == len(GROUPS) - 1 else nc.scalar.copy

            turned = psum.tile([P, n, 2, C], F32, name="turned")
            for k, e in enumerate(GROUPS[g]):
                words = h_of[e][:].rearrange("c u p v -> c (u p v)").bitcast(F32)
                for u in range(2):
                    nc.tensor.transpose(turned[:, k, u, :], words[:, u * P : (u + 1) * P], ident[:])
            h_rows = hidden.tile([P, n, C, PACK], BF16, name="h_rows", align_bytes=64)
            empty(h_rows[:].bitcast(F32), turned[:].rearrange("p k u c -> p k c u"))

            h_codes = hidden.tile([P, n * C], U32, name="h_codes", align_bytes=64)
            h_scales = hidden.tile([P, n * C], U8, name="h_scales", align_bytes=64)
            nc.vector.quantize_mx(
                out=h_codes[:].bitcast(FP8X4),
                scales=h_scales[:],
                in_=h_rows[:].rearrange("p k c j -> p (k c j)"),
            )
            y = psum.tile([N, n * C], F32, name="y")
            for k, e in enumerate(GROUPS[g]):
                mine = slice(k * C, (k + 1) * C)
                nc.tensor.matmul_mx(
                    out=y[:, mine],
                    lhsT=w2_sb[:, e, :].bitcast(FP4X4),
                    lhsT_scale=s2[:, e, :],
                    rhs=h_codes[:, mine].bitcast(FP8X4),
                    rhs_scale=h_scales[:, mine],
                    start=True,
                    stop=True,
                )
            empty(y_all[:, e0 * C : (e0 + n) * C], y[:])

        fetched = 0
        for g in range(len(GROUPS)):
            ahead = GROUPS[min(g + 1, len(GROUPS) - 1)][-1]
            for e0, e1 in PIECES:
                if fetched == e0 and e0 <= ahead:
                    gather(e0, e1)
                    fetched = e1
            first_layer(g)
            if g > 0:
                second_layer(g - 1)
        second_layer(len(GROUPS) - 1)

        parts = [held.tile([N, T], F32, name=f"part_{r}") for r in range(TOP)]
        for r in range(TOP):
            nc.vector.tensor_tensor(parts[r][:], y_all[:].indirect(pos_sb[r][:]), gate_sb[:, r, :], MULT)
        two = held.tile([N, T], F32, name="two")
        total = held.tile([N, T], F32, name="total")
        nc.vector.tensor_tensor(two[:], parts[0][:], parts[1][:], ADD)
        for t0, t1 in ((0, CUT), (CUT, T)):
            nc.vector.tensor_tensor(total[:, t0:t1], two[:, t0:t1], parts[2][:, t0:t1], ADD)
            nc.sync.dma_start(out[:, t0:t1], total[:, t0:t1])
